import numpy as np
import ml_dtypes


def mxq(x, axis, fmt="e4m3"):
    dtype, down = {"e4m3": (ml_dtypes.float8_e4m3fn, 7), "e5m2": (ml_dtypes.float8_e5m2, 14)}[fmt]
    v = np.moveaxis(np.asarray(x, np.float32).astype(ml_dtypes.bfloat16).astype(np.float64), axis, -1)
    blocks = v.reshape(v.shape[:-1] + (-1, 32))
    amax = np.abs(blocks).max(-1, keepdims=True)
    byte = np.maximum(np.where(amax > 0, np.frexp(amax)[1] - 1 + 127, 0) - down, 1)
    scale = np.exp2(byte - 127.0)
    codes = (blocks / scale).astype(np.float32).astype(dtype).astype(np.float64)
    return np.moveaxis((codes * scale).reshape(v.shape), -1, axis)


WIDE = False


def mx_kscale(k, group=512):
    if not WIDE:
        return np.ones(k)
    levels = np.array([18, -18])
    if group != 512:
        return np.exp2(np.random.permutation(np.resize(levels, k // group))).repeat(group)
    if k % 512:
        return np.exp2(np.random.permutation(np.resize(levels, k // 32))).repeat(32)
    a = np.empty((k // 512, 16))
    for p in range(k // 512):
        a[p, :8] = np.random.permutation(np.resize(levels, 8))
        for g in range(8):
            far = levels[np.abs(levels - a[p, g]) >= 10]
            a[p, g + 8] = far[np.random.randint(len(far))]
    return np.exp2(a.ravel()).repeat(32)


def f64(x):
    return np.asarray(x).astype(np.float64)


G, D, M, O, N = 4, 128, 128, 128, 512


def sgn(shape):
    return np.random.uniform(0.5, 2.0, shape) * np.where(np.random.standard_normal(shape) < 0, -1.0, 1.0)


def setup_inputs():
    n = np.random.standard_normal
    s_d = mx_kscale(D, 0)
    s_m = mx_kscale(M, 0)
    return {
        "x": (n((G, D, N)) * s_d[:, None]).astype(np.float32),
        "w1": (n((G, D, M)) / np.sqrt(D) / s_d[:, None]).astype(np.float32),
        "w2": (n((G, D, M)) / np.sqrt(D) / s_d[:, None]).astype(np.float32),
        "sh": (np.random.uniform(0.1, 0.4, (G, M, 1))).astype(np.float32),
        "d0": (np.random.uniform(2.0, 6.0, (G, M, N))).astype(np.float32),
        "hs": (sgn((G, M, 1)) * s_m[:, None]).astype(np.float32),
        "wo2": (n((G, M, O)) / np.sqrt(M) / s_m[:, None]).astype(np.float32),
        "res": (0.5 * n((G, O, N))).astype(np.float32),
    }


def reference(x, w1, w2, sh, d0, hs, wo2, res):
    w1q = mxq(f64(w1), 1, "e4m3")
    xq = mxq(f64(x), 1, "e4m3")
    z1 = w1q.transpose(0, 2, 1) @ xq
    w2q = mxq(f64(w2), 1, "e4m3")
    z2 = w2q.transpose(0, 2, 1) @ xq
    q1 = f64(d0) - z1 * 2.0
    h = np.exp(q1 * f64(sh) * (-1.0)) * z2
    hh = h * f64(hs)
    wo2q = mxq(f64(wo2), 1, "e4m3")
    hhq = mxq(hh, 1, "e4m3")
    y0 = wo2q.transpose(0, 2, 1) @ hhq
    y = y0 + f64(res)
    return y

@@ -1,0 +1,206 @@
+from contextlib import ExitStack
+
+import concourse.mybir as mybir
+
+G, D, M, O, N = 4, 128, 128, 128, 512
+FLOPS = 3 * 2 * G * D * M * N
+
+F32 = mybir.dt.float32
+BF16 = mybir.dt.bfloat16
+U32 = mybir.dt.uint32
+U8 = mybir.dt.uint8
+FP8X4 = mybir.dt.float8_e4m3fn_x4
+ALU = mybir.AluOpType
+ACT = mybir.ActivationFunctionType
+
+P = 128
+PACK = 4
+ROWS = 32
+W = 128
+CHUNKS = N // W
+HALF = N // 2
+RUN = 4
+
+
+def tile_rows_fkernrbf_kernel(tc, x, w1, w2, sh, d0, hs, wo2, res, out):
+    nc = tc.nc
+    with ExitStack() as ctx:
+        sb = ctx.enter_context(tc.tile_pool(name="sb", bufs=1))
+        ps = ctx.enter_context(tc.psum_pool(name="ps", bufs=1))
+        ctx.enter_context(tc.manual_schedule())
+
+        def new(name, shape, dtype):
+            return sb.tile(shape, dtype, name=name, align_bytes=64)
+
+        def rows(g):
+            return slice(ROWS * g, ROWS * (g + 1))
+
+        def cols(c):
+            return slice(W * c, W * (c + 1))
+
+        banks = [[ps.tile([P, 512], F32, name="bank%d_%d" % (g, b)) for b in range(2)] for g in range(G)]
+
+        def packed_rows(t):
+            return t.rearrange("g (p j) n -> (g p) j n", j=PACK)
+
+        def load(name, src):
+            t = new(name, list(src.shape), F32)
+            nc.sync.dma_start(out=t[:], in_=src)
+            return t
+
+        def interleave(name, src, engine):
+            t = new(name, [P, W, PACK], BF16)
+            dst = t[:].rearrange("p (c i) t -> p c t i", i=RUN)
+            walk = src.rearrange("p t (c i) -> p c t i", i=RUN)
+            if engine == "vector":
+                nc.vector.tensor_copy(out=dst, in_=walk)
+            elif engine == "activation":
+                nc.scalar.activation(out=dst, in_=walk, func=ACT.Copy)
+            else:
+                nc.scalar.copy(out=dst, in_=walk)
+            return t
+
+        def quantise(name, t):
+            codes = new(name + "_codes", [P, W], U32)
+            scales = new(name + "_scales", [P, W], U8)
+            nc.vector.quantize_mx(out=codes[:].bitcast(FP8X4), scales=scales[:], in_=t[:].rearrange("p n j -> p (n j)"))
+            return codes, scales
+
+        def product(dst, g, stationary, moving):
+            nc.tensor.matmul_mx(
+                out=dst,
+                lhsT=stationary[0][rows(g), :].bitcast(FP8X4),
+                lhsT_scale=stationary[1][rows(g), :],
+                rhs=moving[0][rows(g), :].bitcast(FP8X4),
+                rhs_scale=moving[1][rows(g), :],
+                start=True,
+                stop=True,
+            )
+
+        vec_rows = new("vec_rows", [P, 2 * G * ROWS], F32)
+        nc.vector.memset(vec_rows[:], 0.0)
+
+        xp = packed_rows(x)
+        d0p = d0.rearrange("g m n -> m g n")
+        resp = res.rearrange("g o n -> o g n")
+        outp = out.rearrange("g o n -> o g n")
+        x_raw = [load("x_raw0", xp[:, :, 0:HALF])]
+        for k, v in enumerate((sh, hs)):
+            nc.sync.dma_start(
+                out=vec_rows[0:P:ROWS, k * P : (k + 1) * P].rearrange("a (g r) -> a g r", g=G),
+                in_=v.rearrange("g (a r) o -> a g (r o)", r=ROWS),
+            )
+        w1_raw = load("w1_raw", packed_rows(w1))
+        w2_raw = load("w2_raw", packed_rows(w2))
+        d0_a = load("d0_a", d0p[:, :, cols(0)])
+        x_raw.append(load("x_raw1", xp[:, :, HALF:N]))
+        d0_b = load("d0_b", d0p[:, :, cols(1)])
+        d0_c = load("d0_c", d0p[:, :, HALF:N])
+        wo2_raw = load("wo2_raw", packed_rows(wo2))
+        d0_of = [d0_a[:], d0_b[:], d0_c[:, :, cols(0)], d0_c[:, :, cols(1)]]
+
+        def x_chunk(c):
+            return x_raw[c // 2][:, :, cols(c % 2)]
+
+        vec_cols = new("vec_cols", [P, 2 * G * ROWS], F32)
+        nc.vector.transpose(vec_cols[:], vec_rows[:])
+
+        def sh_col(g):
+            return vec_cols[:, ROWS * g : ROWS * g + 1]
+
+        def hs_col(g):
+            return vec_cols[:, P + ROWS * g : P + ROWS * g + 1]
+
+        x_il = {}
+        x_q = {}
+        x_il[0] = interleave("x_il0", x_chunk(0), "vector")
+        x_il[1] = interleave("x_il1", x_chunk(1), "activation")
+        w1_il = interleave("w1_il", w1_raw[:], "vector")
+        x_q[0] = quantise("x0", x_il[0])
+        w1_q = quantise("w1", w1_il)
+
+        def z1_of(c, g):
+            return banks[g][c % 2][:, 0:W]
+
+        def z2_of(c, g):
+            return banks[g][c % 2][:, W : 2 * W]
+
+        def y0_of(c, g):
+            return banks[g][c % 2][:, 2 * W : 3 * W]
+
+        def first_products(c):
+            for g in range(G):
+                product(z1_of(c, g), g, w1_q, x_q[c])
+
+        def second_products(c):
+            for g in range(G):
+                product(z2_of(c, g), g, w2_q, x_q[c])
+
+        first_products(0)
+        w2_il = interleave("w2_il", w2_raw[:], "vector")
+        x_q[1] = quantise("x1", x_il[1])
+        w2_q = quantise("w2", w2_il)
+        second_products(0)
+        first_products(1)
+        second_products(1)
+
+        gathered = {}
+        res_half = []
+        for c in range(CHUNKS):
+            negq = new("negq%d" % c, [P, G, W], F32)
+            e = new("e%d" % c, [P, G, W], F32)
+            for g in range(G):
+                nc.vector.scalar_tensor_tensor(
+                    out=negq[:, g, :], in0=z1_of(c, g), scalar=2.0, in1=d0_of[c][:, g, :], op0=ALU.mult, op1=ALU.subtract
+                )
+            for g in range(G):
+                nc.scalar.activation(out=e[:, g, :], in_=negq[:, g, :], func=ACT.Exp, scale=sh_col(g))
+            if 1 <= c < CHUNKS - 1:
+                x_q[c + 1] = quantise("x%d" % (c + 1), x_il[c + 1])
+                first_products(c + 1)
+                second_products(c + 1)
+            if c == CHUNKS - 1:
+                wo2_q = quantise("wo2", wo2_il)
+            if c + 2 < CHUNKS:
+                x_il[c + 2] = interleave("x_il%d" % (c + 2), x_chunk(c + 2), "activation")
+            elif c + 2 == CHUNKS:
+                wo2_il = interleave("wo2_il", wo2_raw[:], "activation")
+            gathered[c] = new("gathered%d" % c, [P, PACK, W], BF16)
+            for g in range(G):
+                hh = new("hh%d_%d" % (c, g), [P, W], BF16)
+                nc.vector.scalar_tensor_tensor(
+                    out=hh[:], in0=z2_of(c, g), scalar=hs_col(g), in1=e[:, g, :], op0=ALU.mult, op1=ALU.mult
+                )
+                nc.sync.dma_start(out=gathered[c][rows(g), :, :], in_=hh[:])
+            if c < 2:
+                res_half.append(load("res%d" % c, resp[:, :, HALF * c : HALF * (c + 1)]))
+
+        y_tiles = [new("y01", [P, G, HALF], F32), new("y2", [P, G, W], F32), new("y3", [P, G, W], F32)]
+        y_of = [y_tiles[0][:, :, cols(0)], y_tiles[0][:, :, cols(1)], y_tiles[1][:], y_tiles[2][:]]
+
+        def third_products(c):
+            hh_il = interleave("hh_il%d" % c, gathered[c][:], "copy")
+            hh_q = quantise("hh%d" % c, hh_il)
+            for g in range(G):
+                product(y0_of(c, g), g, wo2_q, hh_q)
+
+        def add_res(c, groups):
+            for g in groups:
+                nc.vector.tensor_tensor(
+                    out=y_of[c][:, g, :], in0=y0_of(c, g), in1=res_half[c // 2][:, g, cols(c % 2)], op=ALU.add
+                )
+
+        third_products(0)
+        third_products(1)
+        add_res(0, range(G))
+        third_products(2)
+        add_res(1, range(G))
+        nc.sync.dma_start(out=outp[:, :, 0:HALF], in_=y_tiles[0][:])
+        add_res(2, range(0, 2))
+        third_products(3)
+        add_res(2, range(2, G))
+        nc.sync.dma_start(out=outp[:, :, cols(2)], in_=y_tiles[1][:])
+        add_res(3, range(0, 2))
+        nc.sync.dma_start(out=outp[:, 0:2, cols(3)], in_=y_tiles[2][:, 0:2, :])
+        add_res(3, range(2, G))
+        nc.sync.dma_start(out=outp[:, 2:G, cols(3)], in_=y_tiles[2][:, 2:G, :])

@@ -17,7 +17,6 @@ P = 128
 PACK = 4
 ROWS = 32
 W = 128
-CHUNKS = N // W
 HALF = N // 2
 RUN = 4
 
@@ -48,31 +47,35 @@ def tile_rows_fkernrbf_kernel(tc, x, w1, w2, sh, d0, hs, wo2, res, out):
             nc.sync.dma_start(out=t[:], in_=src)
             return t
 
-        def interleave(name, src, engine):
-            t = new(name, [P, W, PACK], BF16)
-            dst = t[:].rearrange("p (c i) t -> p c t i", i=RUN)
+        def interleave(dst, src, engine):
+            dst = dst.rearrange("p (c i) t -> p c t i", i=RUN)
             walk = src.rearrange("p t (c i) -> p c t i", i=RUN)
             if engine == "vector":
                 nc.vector.tensor_copy(out=dst, in_=walk)
             elif engine == "activation":
                 nc.scalar.activation(out=dst, in_=walk, func=ACT.Copy)
+            elif engine == "gpsimd":
+                nc.gpsimd.tensor_scalar(out=dst, in0=walk, scalar1=1.0, scalar2=0.0, op0=ALU.mult, op1=ALU.add)
             else:
                 nc.scalar.copy(out=dst, in_=walk)
-            return t
+
+        def words(name, width):
+            return new(name, [P, width, PACK], BF16)
 
         def quantise(name, t):
-            codes = new(name + "_codes", [P, W], U32)
-            scales = new(name + "_scales", [P, W], U8)
+            width = t.shape[1]
+            codes = new(name + "_codes", [P, width], U32)
+            scales = new(name + "_scales", [P, width], U8)
             nc.vector.quantize_mx(out=codes[:].bitcast(FP8X4), scales=scales[:], in_=t[:].rearrange("p n j -> p (n j)"))
             return codes, scales
 
-        def product(dst, g, stationary, moving):
+        def product(dst, g, stationary, moving, k):
             nc.tensor.matmul_mx(
                 out=dst,
                 lhsT=stationary[0][rows(g), :].bitcast(FP8X4),
                 lhsT_scale=stationary[1][rows(g), :],
-                rhs=moving[0][rows(g), :].bitcast(FP8X4),
-                rhs_scale=moving[1][rows(g), :],
+                rhs=moving[0][rows(g), cols(k)].bitcast(FP8X4),
+                rhs_scale=moving[1][rows(g), cols(k)],
                 start=True,
                 stop=True,
             )
@@ -84,7 +87,7 @@ def tile_rows_fkernrbf_kernel(tc, x, w1, w2, sh, d0, hs, wo2, res, out):
         d0p = d0.rearrange("g m n -> m g n")
         resp = res.rearrange("g o n -> o g n")
         outp = out.rearrange("g o n -> o g n")
-        x_raw = [load("x_raw0", xp[:, :, 0:HALF])]
+        x_lo = load("x_lo", xp[:, :, 0:HALF])
         for k, v in enumerate((sh, hs)):
             nc.sync.dma_start(
                 out=vec_rows[0:P:ROWS, k * P : (k + 1) * P].rearrange("a (g r) -> a g r", g=G),
@@ -92,18 +95,22 @@ def tile_rows_fkernrbf_kernel(tc, x, w1, w2, sh, d0, hs, wo2, res, out):
             )
         w1_raw = load("w1_raw", packed_rows(w1))
         w2_raw = load("w2_raw", packed_rows(w2))
-        d0_a = load("d0_a", d0p[:, :, cols(0)])
-        x_raw.append(load("x_raw1", xp[:, :, HALF:N]))
-        d0_b = load("d0_b", d0p[:, :, cols(1)])
-        d0_c = load("d0_c", d0p[:, :, HALF:N])
+        d0_lo = [load("d0_lo0", d0p[:, 0:2, 0:HALF]), load("d0_lo1", d0p[:, 2:G, 0:HALF])]
+        x_raw = {0: x_lo}
+        d0_hi = {}
+        for c in (1, 2):
+            x_raw[c] = load("x_raw%d" % c, xp[:, :, cols(c + 1)])
+            d0_hi[c] = load("d0_hi%d" % c, d0p[:, :, cols(c + 1)])
         wo2_raw = load("wo2_raw", packed_rows(wo2))
-        d0_of = [d0_a[:], d0_b[:], d0_c[:, :, cols(0)], d0_c[:, :, cols(1)]]
 
-        def x_chunk(c):
-            return x_raw[c // 2][:, :, cols(c % 2)]
+        def d0_of(c, g):
+            return d0_hi[c][:, g, :] if c else d0_lo[g // 2][:, g % 2, :]
+
+        starts = [0, HALF, HALF + W]
+        widths = [HALF, W, W]
+        y_bank = [0, 1, 0]
 
         vec_cols = new("vec_cols", [P, 2 * G * ROWS], F32)
-        nc.vector.transpose(vec_cols[:], vec_rows[:])
 
         def sh_col(g):
             return vec_cols[:, ROWS * g : ROWS * g + 1]
@@ -111,96 +118,119 @@ def tile_rows_fkernrbf_kernel(tc, x, w1, w2, sh, d0, hs, wo2, res, out):
         def hs_col(g):
             return vec_cols[:, P + ROWS * g : P + ROWS * g + 1]
 
-        x_il = {}
-        x_q = {}
-        x_il[0] = interleave("x_il0", x_chunk(0), "vector")
-        x_il[1] = interleave("x_il1", x_chunk(1), "activation")
-        w1_il = interleave("w1_il", w1_raw[:], "vector")
-        x_q[0] = quantise("x0", x_il[0])
-        w1_q = quantise("w1", w1_il)
-
         def z1_of(c, g):
-            return banks[g][c % 2][:, 0:W]
+            return banks[g][0][:, starts[c] : starts[c] + widths[c]]
 
         def z2_of(c, g):
-            return banks[g][c % 2][:, W : 2 * W]
+            return banks[g][1][:, starts[c] : starts[c] + widths[c]]
 
         def y0_of(c, g):
-            return banks[g][c % 2][:, 2 * W : 3 * W]
+            return banks[g][y_bank[c]][:, 0 : widths[c]]
 
-        def first_products(c):
+        def products(dst_of, c, stationary, moving, width):
             for g in range(G):
-                product(z1_of(c, g), g, w1_q, x_q[c])
+                for k in range(width // W):
+                    product(dst_of(c, g)[:, cols(k)], g, stationary, moving, k)
 
-        def second_products(c):
-            for g in range(G):
-                product(z2_of(c, g), g, w2_q, x_q[c])
-
-        first_products(0)
-        w2_il = interleave("w2_il", w2_raw[:], "vector")
-        x_q[1] = quantise("x1", x_il[1])
+        x_il = [words("x_il%d" % c, widths[c]) for c in range(3)]
+        interleave(x_il[0][:, cols(0), :], x_lo[:, :, cols(0)], "vector")
+        interleave(x_il[0][:, cols(1), :], x_lo[:, :, cols(1)], "activation")
+        w1_il = words("w1_il", M)
+        interleave(w1_il[:], w1_raw[:], "vector")
+        w2_il = words("w2_il", M)
+        interleave(w2_il[:], w2_raw[:], "activation")
+        x_q = quantise("x0", x_il[0])
+        w1_q = quantise("w1", w1_il)
+        products(z1_of, 0, w1_q, x_q, HALF)
+        nc.vector.transpose(vec_cols[:], vec_rows[:])
         w2_q = quantise("w2", w2_il)
-        second_products(0)
-        first_products(1)
-        second_products(1)
+        products(z2_of, 0, w2_q, x_q, HALF)
 
-        gathered = {}
-        res_half = []
-        for c in range(CHUNKS):
-            negq = new("negq%d" % c, [P, G, W], F32)
-            e = new("e%d" % c, [P, G, W], F32)
-            for g in range(G):
+        gathered = [new("gathered%d" % c, [P, PACK, widths[c]], BF16) for c in range(3)]
+        negq = {}
+        e = {}
+
+        def distance(c, groups):
+            for g in groups:
+                negq[c, g] = new("negq%d_%d" % (c, g), [P, widths[c]], F32)
                 nc.vector.scalar_tensor_tensor(
-                    out=negq[:, g, :], in0=z1_of(c, g), scalar=2.0, in1=d0_of[c][:, g, :], op0=ALU.mult, op1=ALU.subtract
+                    out=negq[c, g][:],
+                    in0=z1_of(c, g),
+                    scalar=2.0,
+                    in1=d0_of(c, g),
+                    op0=ALU.mult,
+                    op1=ALU.subtract,
                 )
-            for g in range(G):
-                nc.scalar.activation(out=e[:, g, :], in_=negq[:, g, :], func=ACT.Exp, scale=sh_col(g))
-            if 1 <= c < CHUNKS - 1:
-                x_q[c + 1] = quantise("x%d" % (c + 1), x_il[c + 1])
-                first_products(c + 1)
-                second_products(c + 1)
-            if c == CHUNKS - 1:
-                wo2_q = quantise("wo2", wo2_il)
-            if c + 2 < CHUNKS:
-                x_il[c + 2] = interleave("x_il%d" % (c + 2), x_chunk(c + 2), "activation")
-            elif c + 2 == CHUNKS:
-                wo2_il = interleave("wo2_il", wo2_raw[:], "activation")
-            gathered[c] = new("gathered%d" % c, [P, PACK, W], BF16)
-            for g in range(G):
-                hh = new("hh%d_%d" % (c, g), [P, W], BF16)
+
+        def kernel_values(c, groups):
+            for g in groups:
+                e[c, g] = new("e%d_%d" % (c, g), [P, widths[c]], F32)
+                nc.scalar.activation(out=e[c, g][:], in_=negq[c, g][:], func=ACT.Exp, scale=sh_col(g))
+
+        def weigh(c, groups):
+            for g in groups:
+                hh = new("hh%d_%d" % (c, g), [P, widths[c]], BF16)
                 nc.vector.scalar_tensor_tensor(
-                    out=hh[:], in0=z2_of(c, g), scalar=hs_col(g), in1=e[:, g, :], op0=ALU.mult, op1=ALU.mult
+                    out=hh[:], in0=z2_of(c, g), scalar=hs_col(g), in1=e[c, g][:], op0=ALU.mult, op1=ALU.mult
                 )
                 nc.sync.dma_start(out=gathered[c][rows(g), :, :], in_=hh[:])
-            if c < 2:
-                res_half.append(load("res%d" % c, resp[:, :, HALF * c : HALF * (c + 1)]))
 
-        y_tiles = [new("y01", [P, G, HALF], F32), new("y2", [P, G, W], F32), new("y3", [P, G, W], F32)]
-        y_of = [y_tiles[0][:, :, cols(0)], y_tiles[0][:, :, cols(1)], y_tiles[1][:], y_tiles[2][:]]
+        def load_res(c):
+            return load("res%d" % c, resp[:, :, starts[c] : starts[c] + widths[c]])
 
-        def third_products(c):
-            hh_il = interleave("hh_il%d" % c, gathered[c][:], "copy")
-            hh_q = quantise("hh%d" % c, hh_il)
-            for g in range(G):
-                product(y0_of(c, g), g, wo2_q, hh_q)
+        y = [new("y%d" % c, [P, G, widths[c]], F32) for c in range(3)]
+        hh_il = [words("hh_il%d" % c, widths[c]) for c in range(3)]
+
+        def second_layer_products(c):
+            products(y0_of, c, wo2_q, quantise("hh%d" % c, hh_il[c]), widths[c])
 
         def add_res(c, groups):
             for g in groups:
-                nc.vector.tensor_tensor(
-                    out=y_of[c][:, g, :], in0=y0_of(c, g), in1=res_half[c // 2][:, g, cols(c % 2)], op=ALU.add
-                )
+                nc.vector.tensor_tensor(out=y[c][:, g, :], in0=y0_of(c, g), in1=res_of[c][:, g, :], op=ALU.add)
 
-        third_products(0)
-        third_products(1)
-        add_res(0, range(G))
-        third_products(2)
-        add_res(1, range(G))
-        nc.sync.dma_start(out=outp[:, :, 0:HALF], in_=y_tiles[0][:])
+        def store(c, g0, g1):
+            nc.sync.dma_start(out=outp[:, g0:g1, starts[c] : starts[c] + widths[c]], in_=y[c][:, g0:g1, :])
+
+        distance(0, range(G))
+        kernel_values(0, range(0, 2))
+        interleave(x_il[1][:], x_raw[1][:], "activation")
+        kernel_values(0, range(2, G))
+        weigh(0, range(0, 2))
+        x_q = quantise("x1", x_il[1])
+        products(z1_of, 1, w1_q, x_q, W)
+        weigh(0, range(2, G))
+        products(z2_of, 1, w2_q, x_q, W)
+        res_of = [load_res(0)]
+        interleave(x_il[2][:], x_raw[2][:], "activation")
+        distance(1, range(G))
+        kernel_values(1, range(G))
+        x_q = quantise("x2", x_il[2])
+        products(z1_of, 2, w1_q, x_q, W)
+        weigh(1, range(G))
+        res_of.append(load_res(1))
+        products(z2_of, 2, w2_q, x_q, W)
+        wo2_il = words("wo2_il", O)
+        interleave(wo2_il[:], wo2_raw[:], "activation")
+        distance(2, range(G))
+        kernel_values(2, range(G))
+        interleave(hh_il[0][:, cols(1), :], gathered[0][:, :, cols(1)], "copy")
+        weigh(2, range(G))
+        res_of.append(load_res(2))
+        interleave(hh_il[0][:, cols(0), :], gathered[0][:, :, cols(0)], "vector")
+        wo2_q = quantise("wo2", wo2_il)
+        second_layer_products(0)
+        interleave(hh_il[1][:], gathered[1][:], "copy")
+        interleave(hh_il[2][:], gathered[2][:], "copy")
+        add_res(0, range(0, 2))
+        store(0, 0, 2)
+        second_layer_products(1)
+        add_res(0, range(2, G))
+        store(0, 2, G)
+        add_res(1, range(0, 2))
+        second_layer_products(2)
+        add_res(1, range(2, G))
+        store(1, 0, G)
         add_res(2, range(0, 2))
-        third_products(3)
+        store(2, 0, 2)
         add_res(2, range(2, G))
-        nc.sync.dma_start(out=outp[:, :, cols(2)], in_=y_tiles[1][:])
-        add_res(3, range(0, 2))
-        nc.sync.dma_start(out=outp[:, 0:2, cols(3)], in_=y_tiles[2][:, 0:2, :])
-        add_res(3, range(2, G))
-        nc.sync.dma_start(out=outp[:, 2:G, cols(3)], in_=y_tiles[2][:, 2:G, :])
+        store(2, 2, G)

@@ -19,6 +19,8 @@ ROWS = 32
 W = 128
 HALF = N // 2
 RUN = 4
+EVEN, ODD = [0, 2], [1, 3]
+ORDER = EVEN + ODD
 
 
 def tile_rows_fkernrbf_kernel(tc, x, w1, w2, sh, d0, hs, wo2, res, out):
@@ -95,7 +97,7 @@ def tile_rows_fkernrbf_kernel(tc, x, w1, w2, sh, d0, hs, wo2, res, out):
             )
         w1_raw = load("w1_raw", packed_rows(w1))
         w2_raw = load("w2_raw", packed_rows(w2))
-        d0_lo = [load("d0_lo0", d0p[:, 0:2, 0:HALF]), load("d0_lo1", d0p[:, 2:G, 0:HALF])]
+        d0_lo = [load("d0_lo%d" % i, d0p[:, i:G:2, 0:HALF]) for i in range(2)]
         x_raw = {0: x_lo}
         d0_hi = {}
         for c in (1, 2):
@@ -104,10 +106,12 @@ def tile_rows_fkernrbf_kernel(tc, x, w1, w2, sh, d0, hs, wo2, res, out):
         wo2_raw = load("wo2_raw", packed_rows(wo2))
 
         def d0_of(c, g):
-            return d0_hi[c][:, g, :] if c else d0_lo[g // 2][:, g % 2, :]
+            return d0_hi[c][:, g, :] if c else d0_lo[g % 2][:, g // 2, :]
 
         starts = [0, HALF, HALF + W]
         widths = [HALF, W, W]
+        z1_bank = [0, 0, 1]
+        z2_bank = [1, 0, 1]
         y_bank = [0, 1, 0]
 
         vec_cols = new("vec_cols", [P, 2 * G * ROWS], F32)
@@ -119,16 +123,16 @@ def tile_rows_fkernrbf_kernel(tc, x, w1, w2, sh, d0, hs, wo2, res, out):
             return vec_cols[:, P + ROWS * g : P + ROWS * g + 1]
 
         def z1_of(c, g):
-            return banks[g][0][:, starts[c] : starts[c] + widths[c]]
+            return banks[g][z1_bank[c]][:, 0 : widths[c]]
 
         def z2_of(c, g):
-            return banks[g][1][:, starts[c] : starts[c] + widths[c]]
+            return banks[g][z2_bank[c]][:, HALF : HALF + widths[c]]
 
         def y0_of(c, g):
             return banks[g][y_bank[c]][:, 0 : widths[c]]
 
-        def products(dst_of, c, stationary, moving, width):
-            for g in range(G):
+        def products(dst_of, c, stationary, moving, width, groups=ORDER):
+            for g in groups:
                 for k in range(width // W):
                     product(dst_of(c, g)[:, cols(k)], g, stationary, moving, k)
 
@@ -178,7 +182,7 @@ def tile_rows_fkernrbf_kernel(tc, x, w1, w2, sh, d0, hs, wo2, res, out):
         def load_res(c):
             return load("res%d" % c, resp[:, :, starts[c] : starts[c] + widths[c]])
 
-        y = [new("y%d" % c, [P, G, widths[c]], F32) for c in range(3)]
+        y = [[new("y%d_%d" % (c, i), [P, 2, widths[c]], F32) for i in range(2)] for c in range(3)]
         hh_il = [words("hh_il%d" % c, widths[c]) for c in range(3)]
 
         def second_layer_products(c):
@@ -186,51 +190,55 @@ def tile_rows_fkernrbf_kernel(tc, x, w1, w2, sh, d0, hs, wo2, res, out):
 
         def add_res(c, groups):
             for g in groups:
-                nc.vector.tensor_tensor(out=y[c][:, g, :], in0=y0_of(c, g), in1=res_of[c][:, g, :], op=ALU.add)
+                nc.vector.tensor_tensor(out=y[c][g % 2][:, g // 2, :], in0=y0_of(c, g), in1=res_of[c][:, g, :], op=ALU.add)
 
-        def store(c, g0, g1):
-            nc.sync.dma_start(out=outp[:, g0:g1, starts[c] : starts[c] + widths[c]], in_=y[c][:, g0:g1, :])
+        def store(c, i):
+            nc.sync.dma_start(out=outp[:, i:G:2, starts[c] : starts[c] + widths[c]], in_=y[c][i][:])
 
-        distance(0, range(G))
-        kernel_values(0, range(0, 2))
+        def first_layer_products(c):
+            x_q = quantise("x%d" % c, x_il[c])
+            for g in ORDER:
+                product(z1_of(c, g), g, w1_q, x_q, 0)
+                product(z2_of(c, g), g, w2_q, x_q, 0)
+
+        distance(0, ORDER)
+        kernel_values(0, EVEN)
         interleave(x_il[1][:], x_raw[1][:], "activation")
-        kernel_values(0, range(2, G))
-        weigh(0, range(0, 2))
-        x_q = quantise("x1", x_il[1])
-        products(z1_of, 1, w1_q, x_q, W)
-        weigh(0, range(2, G))
-        products(z2_of, 1, w2_q, x_q, W)
+        kernel_values(0, ODD)
+        weigh(0, EVEN)
+        first_layer_products(1)
+        weigh(0, ODD)
         res_of = [load_res(0)]
         interleave(x_il[2][:], x_raw[2][:], "activation")
-        distance(1, range(G))
-        kernel_values(1, range(G))
-        x_q = quantise("x2", x_il[2])
-        products(z1_of, 2, w1_q, x_q, W)
-        weigh(1, range(G))
+        distance(1, EVEN)
+        first_layer_products(2)
+        distance(1, ODD)
+        kernel_values(1, ORDER)
+        weigh(1, ORDER)
         res_of.append(load_res(1))
-        products(z2_of, 2, w2_q, x_q, W)
         wo2_il = words("wo2_il", O)
         interleave(wo2_il[:], wo2_raw[:], "activation")
-        distance(2, range(G))
-        kernel_values(2, range(G))
+        distance(2, ORDER)
+        kernel_values(2, ORDER)
         interleave(hh_il[0][:, cols(1), :], gathered[0][:, :, cols(1)], "copy")
-        weigh(2, range(G))
+        weigh(2, ORDER)
         res_of.append(load_res(2))
         interleave(hh_il[0][:, cols(0), :], gathered[0][:, :, cols(0)], "vector")
         wo2_q = quantise("wo2", wo2_il)
         second_layer_products(0)
         interleave(hh_il[1][:], gathered[1][:], "copy")
         interleave(hh_il[2][:], gathered[2][:], "copy")
-        add_res(0, range(0, 2))
-        store(0, 0, 2)
+        add_res(0, EVEN)
+        store(0, 0)
         second_layer_products(1)
-        add_res(0, range(2, G))
-        store(0, 2, G)
-        add_res(1, range(0, 2))
+        add_res(0, ODD)
+        store(0, 1)
+        add_res(1, EVEN)
+        store(1, 0)
         second_layer_products(2)
-        add_res(1, range(2, G))
-        store(1, 0, G)
-        add_res(2, range(0, 2))
-        store(2, 0, 2)
-        add_res(2, range(2, G))
-        store(2, 2, G)
+        add_res(1, ODD)
+        store(1, 1)
+        add_res(2, EVEN)
+        store(2, 0)
+        add_res(2, ODD)
+        store(2, 1)

@@ -16,11 +16,15 @@ ACT = mybir.ActivationFunctionType
 P = 128
 PACK = 4
 ROWS = 32
-W = 128
+BANK = 512
+QUARTER = N // 4
 HALF = N // 2
 RUN = 4
+
 EVEN, ODD = [0, 2], [1, 3]
 ORDER = EVEN + ODD
+
+SPANS = [slice(0, HALF), slice(HALF, HALF + QUARTER), slice(HALF + QUARTER, N)]
 
 
 def tile_rows_fkernrbf_kernel(tc, x, w1, w2, sh, d0, hs, wo2, res, out):
@@ -36,209 +40,183 @@ def tile_rows_fkernrbf_kernel(tc, x, w1, w2, sh, d0, hs, wo2, res, out):
         def rows(g):
             return slice(ROWS * g, ROWS * (g + 1))
 
-        def cols(c):
-            return slice(W * c, W * (c + 1))
+        def quarter(k):
+            return slice(QUARTER * k, QUARTER * (k + 1))
 
-        banks = [[ps.tile([P, 512], F32, name="bank%d_%d" % (g, b)) for b in range(2)] for g in range(G)]
+        def half(h):
+            return slice(HALF * h, HALF * (h + 1))
 
-        def packed_rows(t):
-            return t.rearrange("g (p j) n -> (g p) j n", j=PACK)
+        def width(span):
+            return span.stop - span.start
 
         def load(name, src):
             t = new(name, list(src.shape), F32)
             nc.sync.dma_start(out=t[:], in_=src)
             return t
 
-        def interleave(dst, src, engine):
-            dst = dst.rearrange("p (c i) t -> p c t i", i=RUN)
-            walk = src.rearrange("p t (c i) -> p c t i", i=RUN)
-            if engine == "vector":
-                nc.vector.tensor_copy(out=dst, in_=walk)
-            elif engine == "activation":
-                nc.scalar.activation(out=dst, in_=walk, func=ACT.Copy)
-            elif engine == "gpsimd":
-                nc.gpsimd.tensor_scalar(out=dst, in0=walk, scalar1=1.0, scalar2=0.0, op0=ALU.mult, op1=ALU.add)
-            else:
-                nc.scalar.copy(out=dst, in_=walk)
+        def by_row_tile(t):
+            return t.rearrange("g (p t) c -> (g p) t c", t=PACK)
 
-        def words(name, width):
-            return new(name, [P, width, PACK], BF16)
+        def interleaved(name, columns):
+            return new(name, [P, columns, PACK], BF16)
+
+        def walk(dst, src):
+            return dst.rearrange("p (c i) t -> p c t i", i=RUN), src.rearrange("p t (c i) -> p c t i", i=RUN)
+
+        def interleave_on_vector(dst, src):
+            dst, src = walk(dst, src)
+            nc.vector.tensor_copy(out=dst, in_=src)
+
+        def round_and_interleave_on_scalar(dst, src):
+            dst, src = walk(dst, src)
+            nc.scalar.activation(out=dst, in_=src, func=ACT.Copy)
+
+        def interleave_on_scalar(dst, src):
+            dst, src = walk(dst, src)
+            nc.scalar.copy(out=dst, in_=src)
 
         def quantise(name, t):
-            width = t.shape[1]
-            codes = new(name + "_codes", [P, width], U32)
-            scales = new(name + "_scales", [P, width], U8)
-            nc.vector.quantize_mx(out=codes[:].bitcast(FP8X4), scales=scales[:], in_=t[:].rearrange("p n j -> p (n j)"))
+            columns = t.shape[1]
+            codes = new(name + "_codes", [P, columns], U32)
+            scales = new(name + "_scales", [P, columns], U8)
+            nc.vector.quantize_mx(out=codes[:].bitcast(FP8X4), scales=scales[:], in_=t[:].rearrange("p c t -> p (c t)"))
             return codes, scales
 
-        def product(dst, g, stationary, moving, k):
-            nc.tensor.matmul_mx(
-                out=dst,
-                lhsT=stationary[0][rows(g), :].bitcast(FP8X4),
-                lhsT_scale=stationary[1][rows(g), :],
-                rhs=moving[0][rows(g), cols(k)].bitcast(FP8X4),
-                rhs_scale=moving[1][rows(g), cols(k)],
-                start=True,
-                stop=True,
-            )
+        def products(dst_of, weights, moving):
+            for k in range(moving[0].shape[1] // QUARTER):
+                for g in ORDER:
+                    nc.tensor.matmul_mx(
+                        out=dst_of(g)[:, quarter(k)],
+                        lhsT=weights[0][rows(g), :].bitcast(FP8X4),
+                        lhsT_scale=weights[1][rows(g), :],
+                        rhs=moving[0][rows(g), quarter(k)].bitcast(FP8X4),
+                        rhs_scale=moving[1][rows(g), quarter(k)],
+                        start=True,
+                        stop=True,
+                    )
+
+        banks = [[ps.tile([P, BANK], F32, name="bank%d_%d" % (g, b)) for b in range(2)] for g in range(G)]
+
+        def z1_of(g):
+            return banks[g][0][:, 0:HALF]
+
+        def z2_of(g):
+            return banks[g][1][:, HALF:BANK]
+
+        def y0_of(s, g):
+            return banks[g][s % 2][:, 0 : width(SPANS[s])]
 
         vec_rows = new("vec_rows", [P, 2 * G * ROWS], F32)
-        nc.vector.memset(vec_rows[:], 0.0)
-
-        xp = packed_rows(x)
-        d0p = d0.rearrange("g m n -> m g n")
-        resp = res.rearrange("g o n -> o g n")
-        outp = out.rearrange("g o n -> o g n")
-        x_lo = load("x_lo", xp[:, :, 0:HALF])
-        for k, v in enumerate((sh, hs)):
-            nc.sync.dma_start(
-                out=vec_rows[0:P:ROWS, k * P : (k + 1) * P].rearrange("a (g r) -> a g r", g=G),
-                in_=v.rearrange("g (a r) o -> a g (r o)", r=ROWS),
-            )
-        w1_raw = load("w1_raw", packed_rows(w1))
-        w2_raw = load("w2_raw", packed_rows(w2))
-        d0_lo = [load("d0_lo%d" % i, d0p[:, i:G:2, 0:HALF]) for i in range(2)]
-        x_raw = {0: x_lo}
-        d0_hi = {}
-        for c in (1, 2):
-            x_raw[c] = load("x_raw%d" % c, xp[:, :, cols(c + 1)])
-            d0_hi[c] = load("d0_hi%d" % c, d0p[:, :, cols(c + 1)])
-        wo2_raw = load("wo2_raw", packed_rows(wo2))
-
-        def d0_of(c, g):
-            return d0_hi[c][:, g, :] if c else d0_lo[g % 2][:, g // 2, :]
-
-        starts = [0, HALF, HALF + W]
-        widths = [HALF, W, W]
-        z1_bank = [0, 0, 1]
-        z2_bank = [1, 0, 1]
-        y_bank = [0, 1, 0]
-
         vec_cols = new("vec_cols", [P, 2 * G * ROWS], F32)
+        nc.vector.memset(vec_rows[:], 0.0)
 
         def sh_col(g):
             return vec_cols[:, ROWS * g : ROWS * g + 1]
 
         def hs_col(g):
-            return vec_cols[:, P + ROWS * g : P + ROWS * g + 1]
+            return vec_cols[:, G * ROWS + ROWS * g : G * ROWS + ROWS * g + 1]
 
-        def z1_of(c, g):
-            return banks[g][z1_bank[c]][:, 0 : widths[c]]
+        x_packed = by_row_tile(x)
+        d0_rows = d0.rearrange("g m n -> m g n")
+        res_rows = res.rearrange("g o n -> o g n")
+        out_rows = out.rearrange("g o n -> o g n")
+        x_lo = load("x_lo", x_packed[:, :, half(0)])
+        for i, vec in enumerate((sh, hs)):
+            nc.sync.dma_start(
+                out=vec_rows[0:P:ROWS, i * G * ROWS : (i + 1) * G * ROWS].rearrange("a (g r) -> a g r", g=G),
+                in_=vec.rearrange("g (a r) o -> a g (r o)", r=ROWS),
+            )
+        w1_raw = load("w1_raw", by_row_tile(w1))
+        w2_raw = load("w2_raw", by_row_tile(w2))
+        d0_lo_even = load("d0_lo_even", d0_rows[:, 0:G:2, half(0)])
+        x_hi = load("x_hi", x_packed[:, :, half(1)])
+        d0_lo_odd = load("d0_lo_odd", d0_rows[:, 1:G:2, half(0)])
+        d0_hi = load("d0_hi", d0_rows[:, :, half(1)])
+        wo2_raw = load("wo2_raw", by_row_tile(wo2))
+        d0_of = [
+            [(d0_lo_even, d0_lo_odd)[g % 2][:, g // 2, :] for g in range(G)],
+            [d0_hi[:, g, :] for g in range(G)],
+        ]
 
-        def z2_of(c, g):
-            return banks[g][z2_bank[c]][:, HALF : HALF + widths[c]]
+        minus_q1 = {}
+        kernel = {}
+        gathered = [new("gathered%d" % h, [P, PACK, HALF], BF16) for h in range(2)]
 
-        def y0_of(c, g):
-            return banks[g][y_bank[c]][:, 0 : widths[c]]
-
-        def products(dst_of, c, stationary, moving, width, groups=ORDER):
+        def distances(h, groups):
             for g in groups:
-                for k in range(width // W):
-                    product(dst_of(c, g)[:, cols(k)], g, stationary, moving, k)
+                minus_q1[h, g] = new("minus_q1_%d_%d" % (h, g), [P, HALF], F32)
+                nc.vector.scalar_tensor_tensor(
+                    out=minus_q1[h, g][:], in0=z1_of(g), scalar=2.0, in1=d0_of[h][g], op0=ALU.mult, op1=ALU.subtract
+                )
 
-        x_il = [words("x_il%d" % c, widths[c]) for c in range(3)]
-        interleave(x_il[0][:, cols(0), :], x_lo[:, :, cols(0)], "vector")
-        interleave(x_il[0][:, cols(1), :], x_lo[:, :, cols(1)], "activation")
-        w1_il = words("w1_il", M)
-        interleave(w1_il[:], w1_raw[:], "vector")
-        w2_il = words("w2_il", M)
-        interleave(w2_il[:], w2_raw[:], "activation")
-        x_q = quantise("x0", x_il[0])
-        w1_q = quantise("w1", w1_il)
-        products(z1_of, 0, w1_q, x_q, HALF)
+        def kernel_values(h, groups):
+            for g in groups:
+                kernel[h, g] = new("kernel%d_%d" % (h, g), [P, HALF], F32)
+                nc.scalar.activation(out=kernel[h, g][:], in_=minus_q1[h, g][:], func=ACT.Exp, scale=sh_col(g))
+
+        def weigh_and_move(h, groups):
+            for g in groups:
+                hh = new("hh%d_%d" % (h, g), [P, HALF], BF16)
+                nc.vector.scalar_tensor_tensor(
+                    out=hh[:], in0=z2_of(g), scalar=hs_col(g), in1=kernel[h, g][:], op0=ALU.mult, op1=ALU.mult
+                )
+                nc.sync.dma_start(out=gathered[h][rows(g), :, :], in_=hh[:])
+
+        hh_in = [interleaved("hh_in%d" % s, width(span)) for s, span in enumerate(SPANS)]
+
+        def second_layer(s):
+            products(lambda g: y0_of(s, g), wo2_q, quantise("hh%d" % s, hh_in[s]))
+
+        def add_res_and_store(s, pair):
+            y = new("y%d_%d" % (s, pair[0]), [P, len(pair), width(SPANS[s])], F32)
+            for i, g in enumerate(pair):
+                nc.vector.tensor_tensor(out=y[:, i, :], in0=y0_of(s, g), in1=res_of[s][:, g, :], op=ALU.add)
+            nc.sync.dma_start(out=out_rows[:, pair[0] : G : 2, SPANS[s]], in_=y[:])
+
+        x_lo_in = interleaved("x_lo_in", HALF)
+        interleave_on_vector(x_lo_in[:, quarter(0), :], x_lo[:, :, quarter(0)])
+        round_and_interleave_on_scalar(x_lo_in[:, quarter(1), :], x_lo[:, :, quarter(1)])
+        w1_in = interleaved("w1_in", M)
+        interleave_on_vector(w1_in[:], w1_raw[:])
+        w2_in = interleaved("w2_in", M)
+        round_and_interleave_on_scalar(w2_in[:], w2_raw[:])
+        x_lo_q = quantise("x_lo", x_lo_in)
+        w1_q = quantise("w1", w1_in)
+        products(z1_of, w1_q, x_lo_q)
         nc.vector.transpose(vec_cols[:], vec_rows[:])
-        w2_q = quantise("w2", w2_il)
-        products(z2_of, 0, w2_q, x_q, HALF)
+        w2_q = quantise("w2", w2_in)
+        products(z2_of, w2_q, x_lo_q)
 
-        gathered = [new("gathered%d" % c, [P, PACK, widths[c]], BF16) for c in range(3)]
-        negq = {}
-        e = {}
-
-        def distance(c, groups):
-            for g in groups:
-                negq[c, g] = new("negq%d_%d" % (c, g), [P, widths[c]], F32)
-                nc.vector.scalar_tensor_tensor(
-                    out=negq[c, g][:],
-                    in0=z1_of(c, g),
-                    scalar=2.0,
-                    in1=d0_of(c, g),
-                    op0=ALU.mult,
-                    op1=ALU.subtract,
-                )
-
-        def kernel_values(c, groups):
-            for g in groups:
-                e[c, g] = new("e%d_%d" % (c, g), [P, widths[c]], F32)
-                nc.scalar.activation(out=e[c, g][:], in_=negq[c, g][:], func=ACT.Exp, scale=sh_col(g))
-
-        def weigh(c, groups):
-            for g in groups:
-                hh = new("hh%d_%d" % (c, g), [P, widths[c]], BF16)
-                nc.vector.scalar_tensor_tensor(
-                    out=hh[:], in0=z2_of(c, g), scalar=hs_col(g), in1=e[c, g][:], op0=ALU.mult, op1=ALU.mult
-                )
-                nc.sync.dma_start(out=gathered[c][rows(g), :, :], in_=hh[:])
-
-        def load_res(c):
-            return load("res%d" % c, resp[:, :, starts[c] : starts[c] + widths[c]])
-
-        y = [[new("y%d_%d" % (c, i), [P, 2, widths[c]], F32) for i in range(2)] for c in range(3)]
-        hh_il = [words("hh_il%d" % c, widths[c]) for c in range(3)]
-
-        def second_layer_products(c):
-            products(y0_of, c, wo2_q, quantise("hh%d" % c, hh_il[c]), widths[c])
-
-        def add_res(c, groups):
-            for g in groups:
-                nc.vector.tensor_tensor(out=y[c][g % 2][:, g // 2, :], in0=y0_of(c, g), in1=res_of[c][:, g, :], op=ALU.add)
-
-        def store(c, i):
-            nc.sync.dma_start(out=outp[:, i:G:2, starts[c] : starts[c] + widths[c]], in_=y[c][i][:])
-
-        def first_layer_products(c):
-            x_q = quantise("x%d" % c, x_il[c])
-            for g in ORDER:
-                product(z1_of(c, g), g, w1_q, x_q, 0)
-                product(z2_of(c, g), g, w2_q, x_q, 0)
-
-        distance(0, ORDER)
+        x_hi_in = interleaved("x_hi_in", HALF)
+        distances(0, EVEN)
         kernel_values(0, EVEN)
-        interleave(x_il[1][:], x_raw[1][:], "activation")
+        round_and_interleave_on_scalar(x_hi_in[:, quarter(0), :], x_hi[:, :, quarter(0)])
+        weigh_and_move(0, EVEN)
+        distances(0, ODD)
+        round_and_interleave_on_scalar(x_hi_in[:, quarter(1), :], x_hi[:, :, quarter(1)])
         kernel_values(0, ODD)
-        weigh(0, EVEN)
-        first_layer_products(1)
-        weigh(0, ODD)
-        res_of = [load_res(0)]
-        interleave(x_il[2][:], x_raw[2][:], "activation")
-        distance(1, EVEN)
-        first_layer_products(2)
-        distance(1, ODD)
+        x_hi_q = quantise("x_hi", x_hi_in)
+        products(z1_of, w1_q, x_hi_q)
+        weigh_and_move(0, ODD)
+        products(z2_of, w2_q, x_hi_q)
+        res_lo = load("res_lo", res_rows[:, :, half(0)])
+
+        wo2_in = interleaved("wo2_in", O)
+        distances(1, ORDER)
         kernel_values(1, ORDER)
-        weigh(1, ORDER)
-        res_of.append(load_res(1))
-        wo2_il = words("wo2_il", O)
-        interleave(wo2_il[:], wo2_raw[:], "activation")
-        distance(2, ORDER)
-        kernel_values(2, ORDER)
-        interleave(hh_il[0][:, cols(1), :], gathered[0][:, :, cols(1)], "copy")
-        weigh(2, ORDER)
-        res_of.append(load_res(2))
-        interleave(hh_il[0][:, cols(0), :], gathered[0][:, :, cols(0)], "vector")
-        wo2_q = quantise("wo2", wo2_il)
-        second_layer_products(0)
-        interleave(hh_il[1][:], gathered[1][:], "copy")
-        interleave(hh_il[2][:], gathered[2][:], "copy")
-        add_res(0, EVEN)
-        store(0, 0)
-        second_layer_products(1)
-        add_res(0, ODD)
-        store(0, 1)
-        add_res(1, EVEN)
-        store(1, 0)
-        second_layer_products(2)
-        add_res(1, ODD)
-        store(1, 1)
-        add_res(2, EVEN)
-        store(2, 0)
-        add_res(2, ODD)
-        store(2, 1)
+        round_and_interleave_on_scalar(wo2_in[:], wo2_raw[:])
+        interleave_on_scalar(hh_in[0][:, quarter(1), :], gathered[0][:, :, quarter(1)])
+        weigh_and_move(1, ORDER)
+        res_hi = load("res_hi", res_rows[:, :, half(1)])
+        res_of = [res_lo[:], res_hi[:, :, quarter(0)], res_hi[:, :, quarter(1)]]
+
+        interleave_on_vector(hh_in[0][:, quarter(0), :], gathered[0][:, :, quarter(0)])
+        wo2_q = quantise("wo2", wo2_in)
+        second_layer(0)
+        interleave_on_scalar(hh_in[1][:], gathered[1][:, :, quarter(0)])
+        interleave_on_scalar(hh_in[2][:], gathered[1][:, :, quarter(1)])
+        for s in range(len(SPANS)):
+            add_res_and_store(s, EVEN)
+            if s + 1 < len(SPANS):
+                second_layer(s + 1)
+            add_res_and_store(s, ODD)

from contextlib import ExitStack

import concourse.mybir as mybir

G, D, M, O, N = 4, 128, 128, 128, 512
FLOPS = 3 * 2 * G * D * M * N

F32 = mybir.dt.float32
BF16 = mybir.dt.bfloat16
U32 = mybir.dt.uint32
U8 = mybir.dt.uint8
FP8X4 = mybir.dt.float8_e4m3fn_x4
ALU = mybir.AluOpType
ACT = mybir.ActivationFunctionType

P = 128
PACK = 4
ROWS = 32
BANK = 512
QUARTER = N // 4
HALF = N // 2
RUN = 4

EVEN, ODD = [0, 2], [1, 3]
ORDER = EVEN + ODD

SPANS = [slice(0, HALF), slice(HALF, HALF + QUARTER), slice(HALF + QUARTER, N)]


def tile_rows_fkernrbf_kernel(tc, x, w1, w2, sh, d0, hs, wo2, res, out):
    nc = tc.nc
    with ExitStack() as ctx:
        sb = ctx.enter_context(tc.tile_pool(name="sb", bufs=1))
        ps = ctx.enter_context(tc.psum_pool(name="ps", bufs=1))
        ctx.enter_context(tc.manual_schedule())

        def new(name, shape, dtype):
            return sb.tile(shape, dtype, name=name, align_bytes=64)

        def rows(g):
            return slice(ROWS * g, ROWS * (g + 1))

        def quarter(k):
            return slice(QUARTER * k, QUARTER * (k + 1))

        def half(h):
            return slice(HALF * h, HALF * (h + 1))

        def width(span):
            return span.stop - span.start

        def load(name, src):
            t = new(name, list(src.shape), F32)
            nc.sync.dma_start(out=t[:], in_=src)
            return t

        def by_row_tile(t):
            return t.rearrange("g (p t) c -> (g p) t c", t=PACK)

        def interleaved(name, columns):
            return new(name, [P, columns, PACK], BF16)

        def walk(dst, src):
            return dst.rearrange("p (c i) t -> p c t i", i=RUN), src.rearrange("p t (c i) -> p c t i", i=RUN)

        def interleave_on_vector(dst, src):
            dst, src = walk(dst, src)
            nc.vector.tensor_copy(out=dst, in_=src)

        def round_and_interleave_on_scalar(dst, src):
            dst, src = walk(dst, src)
            nc.scalar.activation(out=dst, in_=src, func=ACT.Copy)

        def interleave_on_scalar(dst, src):
            dst, src = walk(dst, src)
            nc.scalar.copy(out=dst, in_=src)

        def quantise(name, t):
            columns = t.shape[1]
            codes = new(name + "_codes", [P, columns], U32)
            scales = new(name + "_scales", [P, columns], U8)
            nc.vector.quantize_mx(out=codes[:].bitcast(FP8X4), scales=scales[:], in_=t[:].rearrange("p c t -> p (c t)"))
            return codes, scales

        def products(dst_of, weights, moving):
            for k in range(moving[0].shape[1] // QUARTER):
                for g in ORDER:
                    nc.tensor.matmul_mx(
                        out=dst_of(g)[:, quarter(k)],
                        lhsT=weights[0][rows(g), :].bitcast(FP8X4),
                        lhsT_scale=weights[1][rows(g), :],
                        rhs=moving[0][rows(g), quarter(k)].bitcast(FP8X4),
                        rhs_scale=moving[1][rows(g), quarter(k)],
                        start=True,
                        stop=True,
                    )

        banks = [[ps.tile([P, BANK], F32, name="bank%d_%d" % (g, b)) for b in range(2)] for g in range(G)]

        def z1_of(g):
            return banks[g][0][:, 0:HALF]

        def z2_of(g):
            return banks[g][1][:, HALF:BANK]

        def y0_of(s, g):
            return banks[g][s % 2][:, 0 : width(SPANS[s])]

        vec_rows = new("vec_rows", [P, 2 * G * ROWS], F32)
        vec_cols = new("vec_cols", [P, 2 * G * ROWS], F32)
        nc.vector.memset(vec_rows[:], 0.0)

        def sh_col(g):
            return vec_cols[:, ROWS * g : ROWS * g + 1]

        def hs_col(g):
            return vec_cols[:, G * ROWS + ROWS * g : G * ROWS + ROWS * g + 1]

        x_packed = by_row_tile(x)
        d0_rows = d0.rearrange("g m n -> m g n")
        res_rows = res.rearrange("g o n -> o g n")
        out_rows = out.rearrange("g o n -> o g n")
        x_lo = load("x_lo", x_packed[:, :, half(0)])
        for i, vec in enumerate((sh, hs)):
            nc.sync.dma_start(
                out=vec_rows[0:P:ROWS, i * G * ROWS : (i + 1) * G * ROWS].rearrange("a (g r) -> a g r", g=G),
                in_=vec.rearrange("g (a r) o -> a g (r o)", r=ROWS),
            )
        w1_raw = load("w1_raw", by_row_tile(w1))
        w2_raw = load("w2_raw", by_row_tile(w2))
        d0_lo_even = load("d0_lo_even", d0_rows[:, 0:G:2, half(0)])
        x_hi = load("x_hi", x_packed[:, :, half(1)])
        d0_lo_odd = load("d0_lo_odd", d0_rows[:, 1:G:2, half(0)])
        d0_hi = load("d0_hi", d0_rows[:, :, half(1)])
        wo2_raw = load("wo2_raw", by_row_tile(wo2))
        d0_of = [
            [(d0_lo_even, d0_lo_odd)[g % 2][:, g // 2, :] for g in range(G)],
            [d0_hi[:, g, :] for g in range(G)],
        ]

        minus_q1 = {}
        kernel = {}
        gathered = [new("gathered%d" % h, [P, PACK, HALF], BF16) for h in range(2)]

        def distances(h, groups):
            for g in groups:
                minus_q1[h, g] = new("minus_q1_%d_%d" % (h, g), [P, HALF], F32)
                nc.vector.scalar_tensor_tensor(
                    out=minus_q1[h, g][:], in0=z1_of(g), scalar=2.0, in1=d0_of[h][g], op0=ALU.mult, op1=ALU.subtract
                )

        def kernel_values(h, groups):
            for g in groups:
                kernel[h, g] = new("kernel%d_%d" % (h, g), [P, HALF], F32)
                nc.scalar.activation(out=kernel[h, g][:], in_=minus_q1[h, g][:], func=ACT.Exp, scale=sh_col(g))

        def weigh_and_move(h, groups):
            for g in groups:
                hh = new("hh%d_%d" % (h, g), [P, HALF], BF16)
                nc.vector.scalar_tensor_tensor(
                    out=hh[:], in0=z2_of(g), scalar=hs_col(g), in1=kernel[h, g][:], op0=ALU.mult, op1=ALU.mult
                )
                nc.sync.dma_start(out=gathered[h][rows(g), :, :], in_=hh[:])

        hh_in = [interleaved("hh_in%d" % s, width(span)) for s, span in enumerate(SPANS)]

        def second_layer(s):
            products(lambda g: y0_of(s, g), wo2_q, quantise("hh%d" % s, hh_in[s]))

        def add_res_and_store(s, pair):
            y = new("y%d_%d" % (s, pair[0]), [P, len(pair), width(SPANS[s])], F32)
            for i, g in enumerate(pair):
                nc.vector.tensor_tensor(out=y[:, i, :], in0=y0_of(s, g), in1=res_of[s][:, g, :], op=ALU.add)
            nc.sync.dma_start(out=out_rows[:, pair[0] : G : 2, SPANS[s]], in_=y[:])

        x_lo_in = interleaved("x_lo_in", HALF)
        interleave_on_vector(x_lo_in[:, quarter(0), :], x_lo[:, :, quarter(0)])
        round_and_interleave_on_scalar(x_lo_in[:, quarter(1), :], x_lo[:, :, quarter(1)])
        w1_in = interleaved("w1_in", M)
        interleave_on_vector(w1_in[:], w1_raw[:])
        w2_in = interleaved("w2_in", M)
        round_and_interleave_on_scalar(w2_in[:], w2_raw[:])
        x_lo_q = quantise("x_lo", x_lo_in)
        w1_q = quantise("w1", w1_in)
        products(z1_of, w1_q, x_lo_q)
        nc.vector.transpose(vec_cols[:], vec_rows[:])
        w2_q = quantise("w2", w2_in)
        products(z2_of, w2_q, x_lo_q)

        x_hi_in = interleaved("x_hi_in", HALF)
        distances(0, EVEN)
        kernel_values(0, EVEN)
        round_and_interleave_on_scalar(x_hi_in[:, quarter(0), :], x_hi[:, :, quarter(0)])
        weigh_and_move(0, EVEN)
        distances(0, ODD)
        round_and_interleave_on_scalar(x_hi_in[:, quarter(1), :], x_hi[:, :, quarter(1)])
        kernel_values(0, ODD)
        x_hi_q = quantise("x_hi", x_hi_in)
        products(z1_of, w1_q, x_hi_q)
        weigh_and_move(0, ODD)
        products(z2_of, w2_q, x_hi_q)
        res_lo = load("res_lo", res_rows[:, :, half(0)])

        wo2_in = interleaved("wo2_in", O)
        distances(1, ORDER)
        kernel_values(1, ORDER)
        round_and_interleave_on_scalar(wo2_in[:], wo2_raw[:])
        interleave_on_scalar(hh_in[0][:, quarter(1), :], gathered[0][:, :, quarter(1)])
        weigh_and_move(1, ORDER)
        res_hi = load("res_hi", res_rows[:, :, half(1)])
        res_of = [res_lo[:], res_hi[:, :, quarter(0)], res_hi[:, :, quarter(1)]]

        interleave_on_vector(hh_in[0][:, quarter(0), :], gathered[0][:, :, quarter(0)])
        wo2_q = quantise("wo2", wo2_in)
        second_layer(0)
        interleave_on_scalar(hh_in[1][:], gathered[1][:, :, quarter(0)])
        interleave_on_scalar(hh_in[2][:], gathered[1][:, :, quarter(1)])
        for s in range(len(SPANS)):
            add_res_and_store(s, EVEN)
            if s + 1 < len(SPANS):
                second_layer(s + 1)
            add_res_and_store(s, ODD)
